import numpy as np
import ml_dtypes


def mxq(x, axis, fmt="e4m3"):
    dtype, down = {"e4m3": (ml_dtypes.float8_e4m3fn, 7), "e5m2": (ml_dtypes.float8_e5m2, 14)}[fmt]
    v = np.moveaxis(np.asarray(x, np.float32).astype(ml_dtypes.bfloat16).astype(np.float64), axis, -1)
    blocks = v.reshape(v.shape[:-1] + (-1, 32))
    amax = np.abs(blocks).max(-1, keepdims=True)
    byte = np.maximum(np.where(amax > 0, np.frexp(amax)[1] - 1 + 127, 0) - down, 1)
    scale = np.exp2(byte - 127.0)
    codes = (blocks / scale).astype(np.float32).astype(dtype).astype(np.float64)
    return np.moveaxis((codes * scale).reshape(v.shape), -1, axis)


WIDE = False


def mx_kscale(k):
    if not WIDE:
        return np.ones(k)
    levels = np.array([10, -10, 5, -5, 0])
    if k % 512:
        return np.exp2(np.random.permutation(np.resize(levels, k // 32))).repeat(32)
    a = np.empty((k // 512, 16))
    for p in range(k // 512):
        a[p, :8] = np.random.permutation(np.resize(levels, 8))
        for g in range(8):
            far = levels[np.abs(levels - a[p, g]) >= 10]
            a[p, g + 8] = far[np.random.randint(len(far))]
    return np.exp2(a.ravel()).repeat(32)


BF16 = ml_dtypes.bfloat16


def bf(x):
    return np.asarray(x, np.float32).astype(BF16)


def f64(x):
    return np.asarray(x).astype(np.float64)

def planes(Y):
    n, m = Y.shape
    b = f64(bf(Y)).reshape(n // 32, 32, m)
    amax = np.abs(b).max(1)
    byte = np.clip(np.where(amax > 0, np.frexp(amax)[1] - 1 + 127 - 7, 1), 1, 254)
    codes = (b * np.exp2(127.0 - byte)[:, None, :]).reshape(n, m).astype(np.float32).astype(ml_dtypes.float8_e4m3fn).view(np.uint8)
    words = codes.reshape(n // 512, 128, 4, m).transpose(0, 1, 3, 2)
    return np.ascontiguousarray(words), np.ascontiguousarray(byte.astype(np.uint8).reshape(n // 512, 16, m))


POOLS, DATES, PATHS = 2048, 1536, 1024

SWING = 2.0
DRIFT = 3.5


def setup_inputs():
    s = mx_kscale(DATES)
    cash = SWING / np.sqrt(DATES) * np.random.randn(POOLS, DATES) + DRIFT / DATES
    discount = np.exp(-np.abs(np.random.randn(DATES, PATHS)))
    fee = 0.5 * np.exp(0.4 * np.random.randn(PATHS))
    claim = 3.0 * np.exp(0.1 * np.random.randn(POOLS))
    notional = np.exp(0.7 * np.random.randn(POOLS))
    return {
        "cash": bf(cash * s[None, :]),
        "discount": bf(discount / s[:, None]),
        "fee": bf(fee),
        "claim": bf(claim),
        "notional": bf(notional),
    }


def reference(cash, discount, fee, claim, notional):
    value = mxq(f64(cash), 1, "e4m3") @ mxq(f64(discount), 0, "e4m3")
    available = np.maximum(value - f64(fee)[None, :], 0.0)
    y = np.minimum(available, f64(claim)[:, None]) * f64(notional)[:, None]
    Y = y.reshape(POOLS, PATHS)
    words, scales = planes(Y)
    return y, words, scales

@@ -1,0 +1,238 @@
+from contextlib import ExitStack
+
+import concourse.mybir as mybir
+from concourse.masks import make_identity
+
+POOLS, DATES, PATHS = 2048, 1536, 1024
+FLOPS = 2 * POOLS * DATES * PATHS
+
+F32 = mybir.dt.float32
+BF16 = mybir.dt.bfloat16
+I32 = mybir.dt.int32
+U32 = mybir.dt.uint32
+U8 = mybir.dt.uint8
+FP8X4 = mybir.dt.float8_e4m3fn_x4
+ALU = mybir.AluOpType
+ACT = mybir.ActivationFunctionType
+
+P = 128
+PACK = 4
+SPAN = P * PACK
+PASSES = DATES // SPAN
+GROUPS = POOLS // SPAN
+HALF = 512
+HALVES = PATHS // HALF
+RUN = 3
+BANKS_PER_GROUP = PACK * PASSES // 2
+
+HEAD_SPLIT = 320
+NEXT_SPLIT = 384
+OUT_SPLITS = (0, 64, 160, 160, 160, 160, 256, 320)
+SCALE_ON_VECTOR = 30
+SINGLE_TILES = 2
+LOADS = "c00 d00 d10 d20 c01 c02 c03 c10 d01 c11 d11 c12 d21 c13 c20 c21 c22 c23 c30 c31 c32 c33"
+UNITS = [(0, 0), (1, 0), (0, 1), (1, 1), (2, 0), (2, 1), (3, 0), (3, 1)]
+RUNS = {0: 4, 1: 7, 2: 10, 4: 13, 8: 16, 12: 19, 16: 22, 20: 25}
+NEXT_AT = 4
+SCALE_LAG = 2
+GROUP_LAG = 5
+QUANT_LAG = 8
+LAST_SPLIT = 320
+
+
+def tile_senior_tranche_values_g2_kernel(tc, cash, discount, fee, claim, notional, out_0, out_1, out_2):
+    nc = tc.nc
+    with ExitStack() as ctx:
+        keep = ctx.enter_context(tc.tile_pool(name="keep", bufs=1))
+        work = ctx.enter_context(tc.tile_pool(name="work", bufs=3))
+        psum = ctx.enter_context(tc.psum_pool(name="psum", bufs=1))
+        ctx.enter_context(tc.manual_schedule(engines={mybir.EngineType.PE, mybir.EngineType.SP}))
+
+        fee_rows = keep.tile([P, PATHS // P], BF16, name="fee_rows")
+        claim_cols = keep.tile([P, GROUPS, PACK], BF16, name="claim_cols")
+        notional_raw = keep.tile([P, GROUPS, PACK], BF16, name="notional_raw")
+        nc.scalar.dma_start(out=fee_rows[:], in_=fee.rearrange("(p b) -> p b", p=P))
+        nc.scalar.dma_start(out=notional_raw[:], in_=notional.rearrange("(g p t) -> p g t", p=P, t=PACK))
+        nc.scalar.dma_start(out=claim_cols[:], in_=claim.rearrange("(g p t) -> p g t", p=P, t=PACK))
+
+        cash_raw = {}
+        disc_raw = {}
+
+        def load_cash(g, t):
+            raw = keep.tile([P, DATES], BF16, name="cash_raw_%d_%d" % (g, t))
+            rows = cash[g * SPAN:(g + 1) * SPAN, :].rearrange("(p t) k -> p t k", t=PACK)
+            nc.sync.dma_start(out=raw[:], in_=rows[:, t, :])
+            cash_raw[g, t] = raw
+
+        def load_disc(c, h):
+            raw = keep.tile([P, PACK, HALF], BF16, name="disc_raw_%d_%d" % (c, h))
+            rows = discount[c * SPAN:(c + 1) * SPAN, h * HALF:(h + 1) * HALF]
+            nc.sync.dma_start(out=raw[:], in_=rows.rearrange("(p j) n -> p j n", j=PACK))
+            disc_raw[c, h] = raw
+
+        for name in LOADS.split():
+            if name[0] == "d":
+                load_disc(int(name[1]), int(name[2]))
+            else:
+                load_cash(int(name[1]), int(name[2]))
+
+        ident = keep.tile([P, P], F32, name="ident")
+        make_identity(nc, ident[:])
+
+        notional_cols = keep.tile([P, GROUPS * PACK], F32, name="notional_cols")
+        nc.scalar.activation(out=notional_cols[:], in_=notional_raw[:].rearrange("p g t -> p (g t)"), func=ACT.Copy)
+
+        fee_all = keep.tile([P, PATHS], BF16, name="fee_all")
+        fee_bank = psum.tile([P, PACK, P], F32, name="fee_bank", tag="turned", bufs=RUN)
+        fee_words = fee_rows[:].bitcast(F32)
+        for w in range(PACK):
+            nc.tensor.transpose(fee_bank[:, w, :], fee_words[:, w:w + 1].to_broadcast([P, P]), ident[:])
+        nc.scalar.copy(out=fee_all[:].bitcast(F32).rearrange("p (n w) -> p n w", w=PACK),
+                       in_=fee_bank[:].rearrange("p w n -> p n w"))
+
+        def interleave(dst, src, split):
+            width = src.shape[2]
+            for engine_copy, lo, hi in ((nc.vector.tensor_copy, 0, split), (nc.scalar.copy, split, width)):
+                if hi > lo:
+                    engine_copy(out=dst[:, lo:hi, :].rearrange("p (c i) t -> p c t i", i=4),
+                                in_=src[:, :, lo:hi].rearrange("p t (c i) -> p c t i", i=4))
+
+        disc_grouped, disc_codes, disc_scales = {}, {}, {}
+
+        def group_disc(c, h, split):
+            grouped = work.tile([P, HALF, PACK], BF16, name="disc_grouped", align_bytes=64)
+            interleave(grouped, disc_raw[c, h], split)
+            disc_grouped[c, h] = grouped
+
+        def quantise_disc(c, h):
+            codes = keep.tile([P, HALF], U32, name="disc_codes_%d_%d" % (c, h), align_bytes=64)
+            scales = keep.tile([P, HALF], U8, name="disc_scales_%d_%d" % (c, h), align_bytes=64)
+            nc.vector.quantize_mx(out=codes[:].bitcast(FP8X4), scales=scales[:],
+                                  in_=disc_grouped[c, h][:].rearrange("p n t -> p (n t)"))
+            disc_codes[c, h], disc_scales[c, h] = codes, scales
+
+        turned, cash_grouped, cash_codes, cash_scales = {}, {}, {}, {}
+        banks = []
+        for j in range(0, SINGLE_TILES * PASSES, PASSES):
+            banks.extend([(j, j + 1), (j + 2,)])
+        banks.extend((j, j + 1) for j in range(SINGLE_TILES * PASSES, GROUPS * PACK * PASSES, 2))
+        place = {j: (b, s) for b, held in enumerate(banks) for s, j in enumerate(held)}
+
+        def turn_cash(b):
+            bank = psum.tile([P, len(banks[b]), 2, P], F32, name="turned", tag="turned", bufs=RUN)
+            for s, j in enumerate(banks[b]):
+                tile_no, c = divmod(j, PASSES)
+                words = cash_raw[divmod(tile_no, PACK)][:].bitcast(F32)
+                for u in range(2):
+                    nc.tensor.transpose(bank[:, s, u, :], words[:, 256 * c + u:256 * (c + 1):2], ident[:])
+            turned[b] = bank
+
+        def group_cash(b, engine_copy):
+            grouped = work.tile([P, len(banks[b]) * SPAN], BF16, name="cash_grouped", bufs=4, align_bytes=64)
+            engine_copy(out=grouped[:].bitcast(F32).rearrange("p (s r u) -> p s r u", r=P, u=2),
+                        in_=turned[b][:].rearrange("p s u r -> p s r u"))
+            cash_grouped[b] = grouped
+
+        def quantise_cash(b):
+            codes = keep.tile([P, len(banks[b]) * P], U32, name="cash_codes_%d" % b, align_bytes=64)
+            scales = keep.tile([P, len(banks[b]) * P], U8, name="cash_scales_%d" % b, align_bytes=64)
+            nc.vector.quantize_mx(out=codes[:].bitcast(FP8X4), scales=scales[:], in_=cash_grouped[b][:])
+            cash_codes[b], cash_scales[b] = codes, scales
+
+        units = UNITS
+        steps = [(g, h, t) for g, h in units for t in range(PACK)]
+        value, net, capped, y_tiles, y_grouped = {}, {}, {}, {}, {}
+        y_scales = keep.tile([P, PATHS], U8, name="y_scales", align_bytes=64)
+
+        def multiply(i):
+            g, h, t = steps[i]
+            acc = psum.tile([P, HALF], F32, name="acc", tag="acc", bufs=8 - RUN)
+            for c in range(PASSES):
+                b, s = place[(g * PACK + t) * PASSES + c]
+                cols = slice(s * P, (s + 1) * P)
+                nc.tensor.matmul_mx(out=acc[:], lhsT=cash_codes[b][:, cols].bitcast(FP8X4),
+                                    lhsT_scale=cash_scales[b][:, cols], rhs=disc_codes[c, h][:].bitcast(FP8X4),
+                                    rhs_scale=disc_scales[c, h][:], start=(c == 0), stop=(c == PASSES - 1))
+            value[i] = acc
+
+        def subtract_fee(i):
+            g, h, t = steps[i]
+            net[i] = work.tile([P, HALF], F32, name="net")
+            nc.vector.tensor_tensor(out=net[i][:], in0=value[i][:], in1=fee_all[:, h * HALF:(h + 1) * HALF],
+                                    op=ALU.subtract)
+
+        def cap(i):
+            g, h, t = steps[i]
+            capped[i] = work.tile([P, HALF], F32, name="capped", bufs=6)
+            nc.vector.tensor_scalar(out=capped[i][:], in0=net[i][:], scalar1=0.0, scalar2=claim_cols[:, g, t:t + 1],
+                                    op0=ALU.max, op1=ALU.min)
+
+        def scale(i, on_vector):
+            g, h, t = steps[i]
+            if t == 0:
+                y_tiles[g, h] = work.tile([P, PACK, HALF], F32, name="y")
+            column = notional_cols[:, g * PACK + t:g * PACK + t + 1]
+            if on_vector:
+                nc.vector.tensor_scalar(out=y_tiles[g, h][:, t, :], in0=capped[i][:], scalar1=column, scalar2=None,
+                                        op0=ALU.mult)
+            else:
+                nc.scalar.activation(out=y_tiles[g, h][:, t, :], in_=capped[i][:], func=ACT.Copy, scale=column)
+
+        def out_rows(g, h):
+            return out_0[g * SPAN:(g + 1) * SPAN, h * HALF:(h + 1) * HALF].rearrange("(p t) m -> p t m", t=PACK)
+
+        def group_y(g, h, split):
+            y_grouped[g, h] = work.tile([P, HALF, PACK], BF16, name="y_grouped", bufs=2, align_bytes=64)
+            interleave(y_grouped[g, h], y_tiles[g, h], split)
+
+        def quantise_y(g, h):
+            cols = slice(h * HALF, (h + 1) * HALF)
+            codes = work.tile([P, HALF], U32, name="y_codes", align_bytes=64)
+            nc.vector.quantize_mx(out=codes[:].bitcast(FP8X4), scales=y_scales[PACK * g:P, cols],
+                                  in_=y_grouped[g, h][:].rearrange("p n t -> p (n t)"))
+            words = out_1[g].rearrange("p m t -> p (m t)").bitcast(I32)
+            nc.sync.dma_start(out=words[:, cols], in_=codes[:].bitcast(I32))
+
+        def prepare_cash(first, end):
+            for b0 in range(first, end, RUN):
+                run = range(b0, min(b0 + RUN, end))
+                for b in run:
+                    turn_cash(b)
+                for b in run:
+                    group_cash(b, nc.scalar.copy)
+                    quantise_cash(b)
+
+        prepare_cash(0, 2)
+        for c in range(PASSES):
+            group_disc(c, 0, HEAD_SPLIT)
+            quantise_disc(c, 0)
+
+        last = len(steps) - 1
+        done = 2
+        for i in range(last + 1 + QUANT_LAG):
+            if i in RUNS:
+                prepare_cash(done, RUNS[i])
+                done = RUNS[i]
+            if i <= last:
+                multiply(i)
+                subtract_fee(i)
+            if 1 <= i <= last + 1:
+                cap(i - 1)
+            if NEXT_AT <= i < NEXT_AT + PASSES:
+                group_disc(i - NEXT_AT, 1, NEXT_SPLIT)
+                quantise_disc(i - NEXT_AT, 1)
+            if SCALE_LAG <= i <= last + SCALE_LAG:
+                g, h, t = steps[i - SCALE_LAG]
+                scale(i - SCALE_LAG, i - SCALE_LAG >= SCALE_ON_VECTOR)
+                nc.sync.dma_start(out=out_rows(g, h)[:, t, :], in_=y_tiles[g, h][:, t, :])
+            if GROUP_LAG <= i <= last + GROUP_LAG and (i - GROUP_LAG) % PACK == 0:
+                u = (i - GROUP_LAG) // PACK
+                group_y(units[u][0], units[u][1], OUT_SPLITS[u])
+            if QUANT_LAG <= i <= last + QUANT_LAG and (i - QUANT_LAG) % PACK == 0:
+                quantise_y(*units[(i - QUANT_LAG) // PACK])
+
+        scale_rows = out_2.bitcast(I32)
+        for q in range(4):
+            queue = nc.scalar if q < 2 else nc.sync
+            queue.dma_start(out=scale_rows[:, 4 * q:4 * q + 4, :],
+                              in_=y_scales[32 * q:32 * q + 4 * GROUPS, :].bitcast(I32))

@@ -26,17 +26,20 @@ RUN = 3
 BANKS_PER_GROUP = PACK * PASSES // 2
 
 HEAD_SPLIT = 320
-NEXT_SPLIT = 384
-OUT_SPLITS = (0, 64, 160, 160, 160, 160, 256, 320)
+NEXT_SPLIT = 256
+OUT_SPLITS = (96, 96, 96, 96, 96, 64, 0, 320)
 SCALE_ON_VECTOR = 30
-SINGLE_TILES = 2
-LOADS = "c00 d00 d10 d20 c01 c02 c03 c10 d01 c11 d11 c12 d21 c13 c20 c21 c22 c23 c30 c31 c32 c33"
-UNITS = [(0, 0), (1, 0), (0, 1), (1, 1), (2, 0), (2, 1), (3, 0), (3, 1)]
-RUNS = {0: 4, 1: 7, 2: 10, 4: 13, 8: 16, 12: 19, 16: 22, 20: 25}
-NEXT_AT = 4
+SINGLE_TILES = 4
+LOADS = "d00 c00 d10 c01 d20 c02 c03 d01 d11 d21 c10 c11 c12 c13 c20 c21 c22 c23 c30 c31 c32 c33"
+UNITS = [(g, h) for g in range(4) for h in range(2)]
+Q2 = 2
+FEES = (3, 3, 3, 4, 4, 3, 0, 0)
+FIRST_SPLIT = 512
+GROUPV_LAG = 5
 SCALE_LAG = 2
-GROUP_LAG = 5
-QUANT_LAG = 8
+GROUP_LAG = 4
+FEE_BUFS = 14
+QUANT_LAG = 7
 LAST_SPLIT = 320
 
 
@@ -46,13 +49,13 @@ def tile_senior_tranche_values_g2_kernel(tc, cash, discount, fee, claim, notiona
         keep = ctx.enter_context(tc.tile_pool(name="keep", bufs=1))
         work = ctx.enter_context(tc.tile_pool(name="work", bufs=3))
         psum = ctx.enter_context(tc.psum_pool(name="psum", bufs=1))
-        ctx.enter_context(tc.manual_schedule(engines={mybir.EngineType.PE, mybir.EngineType.SP}))
+        ctx.enter_context(tc.manual_schedule())
 
         fee_rows = keep.tile([P, PATHS // P], BF16, name="fee_rows")
         claim_cols = keep.tile([P, GROUPS, PACK], BF16, name="claim_cols")
         notional_raw = keep.tile([P, GROUPS, PACK], BF16, name="notional_raw")
-        nc.scalar.dma_start(out=fee_rows[:], in_=fee.rearrange("(p b) -> p b", p=P))
         nc.scalar.dma_start(out=notional_raw[:], in_=notional.rearrange("(g p t) -> p g t", p=P, t=PACK))
+        nc.scalar.dma_start(out=fee_rows[:], in_=fee.rearrange("(p b) -> p b", p=P))
         nc.scalar.dma_start(out=claim_cols[:], in_=claim.rearrange("(g p t) -> p g t", p=P, t=PACK))
 
         cash_raw = {}
@@ -71,7 +74,13 @@ def tile_senior_tranche_values_g2_kernel(tc, cash, discount, fee, claim, notiona
             disc_raw[c, h] = raw
 
         for name in LOADS.split():
-            if name[0] == "d":
+            if name[0] == "D":
+                c = int(name[1])
+                raw = keep.tile([P, PACK, PATHS], BF16, name="disc_full_%d" % c)
+                nc.sync.dma_start(out=raw[:], in_=discount[c * SPAN:(c + 1) * SPAN, :].rearrange("(p j) n -> p j n", j=PACK))
+                for h in range(HALVES):
+                    disc_raw[c, h] = raw[:, :, h * HALF:(h + 1) * HALF]
+            elif name[0] == "d":
                 load_disc(int(name[1]), int(name[2]))
             else:
                 load_cash(int(name[1]), int(name[2]))
@@ -82,18 +91,33 @@ def tile_senior_tranche_values_g2_kernel(tc, cash, discount, fee, claim, notiona
         notional_cols = keep.tile([P, GROUPS * PACK], F32, name="notional_cols")
         nc.scalar.activation(out=notional_cols[:], in_=notional_raw[:].rearrange("p g t -> p (g t)"), func=ACT.Copy)
 
+        claim_flat = claim_cols[:].rearrange("p g t -> p (g t)")
+        at_claim = keep.tile([P, GROUPS * PACK], F32, name="at_claim")
+        at_floor = keep.tile([P, GROUPS * PACK], F32, name="at_floor")
+        lower = keep.tile([P, GROUPS * PACK], F32, name="lower")
+        upper = keep.tile([P, GROUPS * PACK], F32, name="upper")
+
+        def bounds():
+            nc.vector.tensor_tensor(out=at_claim[:], in0=claim_flat, in1=notional_cols[:], op=ALU.mult)
+            nc.vector.scalar_tensor_tensor(out=at_floor[:], in0=claim_flat, scalar=0.0, in1=notional_cols[:],
+                                           op0=ALU.min, op1=ALU.mult)
+            nc.vector.tensor_tensor(out=lower[:], in0=at_claim[:], in1=at_floor[:], op=ALU.min)
+            nc.vector.tensor_tensor(out=upper[:], in0=at_claim[:], in1=at_floor[:], op=ALU.max)
+
         fee_all = keep.tile([P, PATHS], BF16, name="fee_all")
         fee_bank = psum.tile([P, PACK, P], F32, name="fee_bank", tag="turned", bufs=RUN)
         fee_words = fee_rows[:].bitcast(F32)
         for w in range(PACK):
             nc.tensor.transpose(fee_bank[:, w, :], fee_words[:, w:w + 1].to_broadcast([P, P]), ident[:])
-        nc.scalar.copy(out=fee_all[:].bitcast(F32).rearrange("p (n w) -> p n w", w=PACK),
-                       in_=fee_bank[:].rearrange("p w n -> p n w"))
 
-        def interleave(dst, src, split):
+        def spread_fee():
+            nc.scalar.copy(out=fee_all[:].bitcast(F32).rearrange("p (n w) -> p n w", w=PACK),
+                           in_=fee_bank[:].rearrange("p w n -> p n w"))
+
+        def interleave(dst, src, split, part="sv"):
             width = src.shape[2]
-            for engine_copy, lo, hi in ((nc.vector.tensor_copy, 0, split), (nc.scalar.copy, split, width)):
-                if hi > lo:
+            for engine_copy, lo, hi, who in ((nc.vector.tensor_copy, 0, split, "v"), (nc.scalar.copy, split, width, "s")):
+                if hi > lo and who in part:
                     engine_copy(out=dst[:, lo:hi, :].rearrange("p (c i) t -> p c t i", i=4),
                                 in_=src[:, :, lo:hi].rearrange("p t (c i) -> p c t i", i=4))
 
@@ -128,7 +152,7 @@ def tile_senior_tranche_values_g2_kernel(tc, cash, discount, fee, claim, notiona
             turned[b] = bank
 
         def group_cash(b, engine_copy):
-            grouped = work.tile([P, len(banks[b]) * SPAN], BF16, name="cash_grouped", bufs=4, align_bytes=64)
+            grouped = work.tile([P, len(banks[b]) * SPAN], BF16, name="cash_grouped", bufs=6, align_bytes=64)
             engine_copy(out=grouped[:].bitcast(F32).rearrange("p (s r u) -> p s r u", r=P, u=2),
                         in_=turned[b][:].rearrange("p s u r -> p s r u"))
             cash_grouped[b] = grouped
@@ -155,35 +179,41 @@ def tile_senior_tranche_values_g2_kernel(tc, cash, discount, fee, claim, notiona
                                     rhs_scale=disc_scales[c, h][:], start=(c == 0), stop=(c == PASSES - 1))
             value[i] = acc
 
+        fee_due = {}
+
+        def scale_fee(i, on_vector):
+            g, h, t = steps[i]
+            fee_due[i] = work.tile([P, HALF], F32, name="fee_due", bufs=FEE_BUFS)
+            column = notional_cols[:, g * PACK + t:g * PACK + t + 1]
+            fees = fee_all[:, h * HALF:(h + 1) * HALF]
+            if on_vector:
+                nc.vector.tensor_scalar(out=fee_due[i][:], in0=fees, scalar1=column, scalar2=None, op0=ALU.mult)
+            else:
+                nc.scalar.activation(out=fee_due[i][:], in_=fees, func=ACT.Copy, scale=column)
+
         def subtract_fee(i):
             g, h, t = steps[i]
-            net[i] = work.tile([P, HALF], F32, name="net")
-            nc.vector.tensor_tensor(out=net[i][:], in0=value[i][:], in1=fee_all[:, h * HALF:(h + 1) * HALF],
-                                    op=ALU.subtract)
+            net[i] = work.tile([P, HALF], F32, name="net", bufs=4)
+            nc.vector.scalar_tensor_tensor(out=net[i][:], in0=value[i][:],
+                                           scalar=notional_cols[:, g * PACK + t:g * PACK + t + 1],
+                                           in1=fee_due[i][:], op0=ALU.mult, op1=ALU.subtract)
 
         def cap(i):
             g, h, t = steps[i]
-            capped[i] = work.tile([P, HALF], F32, name="capped", bufs=6)
-            nc.vector.tensor_scalar(out=capped[i][:], in0=net[i][:], scalar1=0.0, scalar2=claim_cols[:, g, t:t + 1],
-                                    op0=ALU.max, op1=ALU.min)
-
-        def scale(i, on_vector):
-            g, h, t = steps[i]
             if t == 0:
                 y_tiles[g, h] = work.tile([P, PACK, HALF], F32, name="y")
-            column = notional_cols[:, g * PACK + t:g * PACK + t + 1]
-            if on_vector:
-                nc.vector.tensor_scalar(out=y_tiles[g, h][:, t, :], in0=capped[i][:], scalar1=column, scalar2=None,
-                                        op0=ALU.mult)
-            else:
-                nc.scalar.activation(out=y_tiles[g, h][:, t, :], in_=capped[i][:], func=ACT.Copy, scale=column)
+            j = g * PACK + t
+            nc.vector.tensor_scalar(out=y_tiles[g, h][:, t, :], in0=net[i][:], scalar1=lower[:, j:j + 1],
+                                    scalar2=upper[:, j:j + 1], op0=ALU.max, op1=ALU.min)
+            nc.sync.dma_start(out=out_rows(g, h)[:, t, :], in_=y_tiles[g, h][:, t, :])
 
         def out_rows(g, h):
             return out_0[g * SPAN:(g + 1) * SPAN, h * HALF:(h + 1) * HALF].rearrange("(p t) m -> p t m", t=PACK)
 
-        def group_y(g, h, split):
-            y_grouped[g, h] = work.tile([P, HALF, PACK], BF16, name="y_grouped", bufs=2, align_bytes=64)
-            interleave(y_grouped[g, h], y_tiles[g, h], split)
+        def group_y(g, h, split, part):
+            if part == "s":
+                y_grouped[g, h] = work.tile([P, HALF, PACK], BF16, name="y_grouped", bufs=2, align_bytes=64)
+            interleave(y_grouped[g, h], y_tiles[g, h], split, part)
 
         def quantise_y(g, h):
             cols = slice(h * HALF, (h + 1) * HALF)
@@ -193,43 +223,101 @@ def tile_senior_tranche_values_g2_kernel(tc, cash, discount, fee, claim, notiona
             words = out_1[g].rearrange("p m t -> p (m t)").bitcast(I32)
             nc.sync.dma_start(out=words[:, cols], in_=codes[:].bitcast(I32))
 
-        def prepare_cash(first, end):
-            for b0 in range(first, end, RUN):
-                run = range(b0, min(b0 + RUN, end))
-                for b in run:
-                    turn_cash(b)
-                for b in run:
-                    group_cash(b, nc.scalar.copy)
-                    quantise_cash(b)
+        def turn_run(first, end):
+            for b in range(first, end):
+                turn_cash(b)
 
-        prepare_cash(0, 2)
-        for c in range(PASSES):
-            group_disc(c, 0, HEAD_SPLIT)
-            quantise_disc(c, 0)
+        def copy_run(first, end):
+            for b in range(first, end):
+                group_cash(b, nc.scalar.copy)
+
+        def quantise_run(first, end):
+            for b in range(first, end):
+                quantise_cash(b)
+
+        group_disc(0, 0, HEAD_SPLIT)
+        spread_fee()
+        turn_run(0, 2)
+        bounds()
+        quantise_disc(0, 0)
+        scale_fee(0, True)
+        scale_fee(1, True)
+        scale_fee(2, False)
+        copy_run(0, 1)
+        group_disc(1, 0, HEAD_SPLIT)
+        copy_run(1, 2)
+        quantise_cash(0)
+        quantise_disc(1, 0)
+        quantise_cash(1)
+        scale_fee(3, False)
+        turn_run(2, 4)
+        group_disc(2, 0, HEAD_SPLIT)
+        copy_run(2, 4)
+        scale_fee(4, True)
+        quantise_disc(2, 0)
+        quantise_run(2, 4)
+        scale_fee(5, True)
+        scale_fee(6, False)
+        scale_fee(7, False)
+        scale_fee(8, False)
+        multiply(0)
+        turn_run(4, 6)
+        copy_run(4, 6)
+        subtract_fee(0)
+        multiply(1)
+        turn_run(6, 8)
+        group_disc(0, 1, FIRST_SPLIT)
+        quantise_run(4, 6)
+        scale_fee(9, False)
+        copy_run(6, 8)
+        quantise_disc(0, 1)
+        subtract_fee(1)
+        multiply(2)
+        quantise_run(6, 8)
+        group_disc(1, 1, NEXT_SPLIT)
+        multiply(3)
+        cap(0)
+        quantise_disc(1, 1)
+        group_disc(2, 1, NEXT_SPLIT)
+        subtract_fee(2)
+        scale_fee(10, False)
+        quantise_disc(2, 1)
+        turn_run(8, 11)
+        copy_run(8, 11)
+        scale_fee(11, False)
+        cap(1)
+        subtract_fee(3)
+        cap(2)
+        multiply(4)
+        subtract_fee(4)
+        cap(3)
+        quantise_run(8, 11)
 
         last = len(steps) - 1
-        done = 2
-        for i in range(last + 1 + QUANT_LAG):
-            if i in RUNS:
-                prepare_cash(done, RUNS[i])
-                done = RUNS[i]
+        for i in range(PACK + 1, last + 1 + PACK + 1):
+            u, t = divmod(i, PACK)
+            first = 11 + RUN * (u - 1)
+            turning = first < len(banks)
+            if t == 1 and turning:
+                turn_run(first, first + RUN)
             if i <= last:
                 multiply(i)
                 subtract_fee(i)
-            if 1 <= i <= last + 1:
+            if i <= last + 1:
                 cap(i - 1)
-            if NEXT_AT <= i < NEXT_AT + PASSES:
-                group_disc(i - NEXT_AT, 1, NEXT_SPLIT)
-                quantise_disc(i - NEXT_AT, 1)
-            if SCALE_LAG <= i <= last + SCALE_LAG:
-                g, h, t = steps[i - SCALE_LAG]
-                scale(i - SCALE_LAG, i - SCALE_LAG >= SCALE_ON_VECTOR)
-                nc.sync.dma_start(out=out_rows(g, h)[:, t, :], in_=y_tiles[g, h][:, t, :])
-            if GROUP_LAG <= i <= last + GROUP_LAG and (i - GROUP_LAG) % PACK == 0:
-                u = (i - GROUP_LAG) // PACK
-                group_y(units[u][0], units[u][1], OUT_SPLITS[u])
-            if QUANT_LAG <= i <= last + QUANT_LAG and (i - QUANT_LAG) % PACK == 0:
-                quantise_y(*units[(i - QUANT_LAG) // PACK])
+            if t == 1:
+                if turning:
+                    copy_run(first, first + RUN)
+                group_y(units[u - 1][0], units[u - 1][1], OUT_SPLITS[u - 1], "s")
+                for j in range(len(fee_due), min(len(fee_due) + FEES[u - 1], last + 1)):
+                    scale_fee(j, False)
+                group_y(units[u - 1][0], units[u - 1][1], OUT_SPLITS[u - 1], "v")
+            if t == 2 and turning:
+                quantise_run(first, first + Q2)
+            if t == 3 and turning:
+                quantise_run(first + Q2, first + 3)
+            if t == 0:
+                quantise_y(*units[u - 2])
 
         scale_rows = out_2.bitcast(I32)
         for q in range(4):

@@ -27,13 +27,14 @@ BANKS_PER_GROUP = PACK * PASSES // 2
 
 HEAD_SPLIT = 320
 NEXT_SPLIT = 256
-OUT_SPLITS = (96, 96, 96, 96, 96, 64, 0, 320)
+OUT_SPLITS = (192, 192, 192, 192, 192, 0, 0, 320)
 SCALE_ON_VECTOR = 30
 SINGLE_TILES = 4
-LOADS = "d00 c00 d10 c01 d20 c02 c03 d01 d11 d21 c10 c11 c12 c13 c20 c21 c22 c23 c30 c31 c32 c33"
+LOADS = "d00 c00 d10 c01 d20 c02 c03 d01 d11 d21 c10 c11 c12 c13 c20 c21 c22 c23"
 UNITS = [(g, h) for g in range(4) for h in range(2)]
-Q2 = 2
-FEES = (3, 3, 3, 4, 4, 3, 0, 0)
+ON_GPSIMD = 2
+G_FROM = 1
+FEES = (3, 3, 4, 4, 4, 2, 0, 0)
 FIRST_SPLIT = 512
 GROUPV_LAG = 5
 SCALE_LAG = 2
@@ -193,25 +194,26 @@ def tile_senior_tranche_values_g2_kernel(tc, cash, discount, fee, claim, notiona
 
         def subtract_fee(i):
             g, h, t = steps[i]
-            net[i] = work.tile([P, HALF], F32, name="net", bufs=4)
+            net[i] = work.tile([P, HALF], F32, name="net", bufs=5)
             nc.vector.scalar_tensor_tensor(out=net[i][:], in0=value[i][:],
                                            scalar=notional_cols[:, g * PACK + t:g * PACK + t + 1],
                                            in1=fee_due[i][:], op0=ALU.mult, op1=ALU.subtract)
 
-        def cap(i):
+        def cap(i, on_gpsimd=False):
             g, h, t = steps[i]
             if t == 0:
                 y_tiles[g, h] = work.tile([P, PACK, HALF], F32, name="y")
             j = g * PACK + t
-            nc.vector.tensor_scalar(out=y_tiles[g, h][:, t, :], in0=net[i][:], scalar1=lower[:, j:j + 1],
-                                    scalar2=upper[:, j:j + 1], op0=ALU.max, op1=ALU.min)
+            engine = nc.gpsimd if on_gpsimd else nc.vector
+            engine.tensor_scalar(out=y_tiles[g, h][:, t, :], in0=net[i][:], scalar1=upper[:, j:j + 1],
+                                 scalar2=lower[:, j:j + 1], op0=ALU.min, op1=ALU.max)
             nc.sync.dma_start(out=out_rows(g, h)[:, t, :], in_=y_tiles[g, h][:, t, :])
 
         def out_rows(g, h):
             return out_0[g * SPAN:(g + 1) * SPAN, h * HALF:(h + 1) * HALF].rearrange("(p t) m -> p t m", t=PACK)
 
         def group_y(g, h, split, part):
-            if part == "s":
+            if "s" in part:
                 y_grouped[g, h] = work.tile([P, HALF, PACK], BF16, name="y_grouped", bufs=2, align_bytes=64)
             interleave(y_grouped[g, h], y_tiles[g, h], split, part)
 
@@ -288,36 +290,37 @@ def tile_senior_tranche_values_g2_kernel(tc, cash, discount, fee, claim, notiona
         cap(1)
         subtract_fee(3)
         cap(2)
-        multiply(4)
-        subtract_fee(4)
         cap(3)
+        for t in range(PACK):
+            load_cash(GROUPS - 1, t)
         quantise_run(8, 11)
 
         last = len(steps) - 1
-        for i in range(PACK + 1, last + 1 + PACK + 1):
-            u, t = divmod(i, PACK)
+        for u in range(1, len(units)):
             first = 11 + RUN * (u - 1)
             turning = first < len(banks)
-            if t == 1 and turning:
-                turn_run(first, first + RUN)
-            if i <= last:
-                multiply(i)
-                subtract_fee(i)
-            if i <= last + 1:
-                cap(i - 1)
-            if t == 1:
-                if turning:
-                    copy_run(first, first + RUN)
-                group_y(units[u - 1][0], units[u - 1][1], OUT_SPLITS[u - 1], "s")
-                for j in range(len(fee_due), min(len(fee_due) + FEES[u - 1], last + 1)):
-                    scale_fee(j, False)
-                group_y(units[u - 1][0], units[u - 1][1], OUT_SPLITS[u - 1], "v")
-            if t == 2 and turning:
-                quantise_run(first, first + Q2)
-            if t == 3 and turning:
-                quantise_run(first + Q2, first + 3)
-            if t == 0:
-                quantise_y(*units[u - 2])
+            for t in range(PACK):
+                if t == 1 and turning:
+                    turn_run(first, first + RUN)
+                multiply(PACK * u + t)
+                subtract_fee(PACK * u + t)
+            for t in range(PACK):
+                cap(PACK * u + t, t < ON_GPSIMD and u >= G_FROM)
+            if u == 1:
+                copy_run(first, first + RUN)
+            group_y(units[u - 1][0], units[u - 1][1], OUT_SPLITS[u - 1], "s")
+            if turning and u > 1:
+                copy_run(first, first + RUN)
+            for j in range(len(fee_due), min(len(fee_due) + FEES[u - 1], last + 1)):
+                scale_fee(j, False)
+            group_y(units[u - 1][0], units[u - 1][1], OUT_SPLITS[u - 1], "v")
+            if turning:
+                quantise_run(first, first + 1)
+            quantise_y(*units[u - 1])
+            if turning:
+                quantise_run(first + 1, first + RUN)
+        group_y(units[-1][0], units[-1][1], OUT_SPLITS[-1], "sv")
+        quantise_y(*units[-1])
 
         scale_rows = out_2.bitcast(I32)
         for q in range(4):

@@ -20,28 +20,21 @@ PACK = 4
 SPAN = P * PACK
 PASSES = DATES // SPAN
 GROUPS = POOLS // SPAN
+TILES = GROUPS * PACK
 HALF = 512
 HALVES = PATHS // HALF
-RUN = 3
-BANKS_PER_GROUP = PACK * PASSES // 2
+UNITS = GROUPS * HALVES
+TURN_BANKS = 3
+SUM_BANKS = 8 - TURN_BANKS
+RUN = 4
 
-HEAD_SPLIT = 320
-NEXT_SPLIT = 256
-OUT_SPLITS = (192, 192, 192, 192, 192, 0, 0, 320)
-SCALE_ON_VECTOR = 30
-SINGLE_TILES = 4
-LOADS = "d00 c00 d10 c01 d20 c02 c03 d01 d11 d21 c10 c11 c12 c13 c20 c21 c22 c23"
-UNITS = [(g, h) for g in range(4) for h in range(2)]
+HEAD_SHARE = 320
+NEXT_SHARE = 320
+OUT_SHARE = 224
+LAST_SHARE = 256
 ON_GPSIMD = 2
-G_FROM = 1
-FEES = (3, 3, 4, 4, 4, 2, 0, 0)
-FIRST_SPLIT = 512
-GROUPV_LAG = 5
-SCALE_LAG = 2
-GROUP_LAG = 4
-FEE_BUFS = 14
-QUANT_LAG = 7
-LAST_SPLIT = 320
+FEE_TILES = 14
+FEES = (4, 4, 4, 4, 4, 3, 0)
 
 
 def tile_senior_tranche_values_g2_kernel(tc, cash, discount, fee, claim, notional, out_0, out_1, out_2):
@@ -52,61 +45,56 @@ def tile_senior_tranche_values_g2_kernel(tc, cash, discount, fee, claim, notiona
         psum = ctx.enter_context(tc.psum_pool(name="psum", bufs=1))
         ctx.enter_context(tc.manual_schedule())
 
-        fee_rows = keep.tile([P, PATHS // P], BF16, name="fee_rows")
-        claim_cols = keep.tile([P, GROUPS, PACK], BF16, name="claim_cols")
         notional_raw = keep.tile([P, GROUPS, PACK], BF16, name="notional_raw")
+        fee_rows = keep.tile([P, PATHS // P], BF16, name="fee_rows")
+        claim_raw = keep.tile([P, GROUPS, PACK], BF16, name="claim_raw")
         nc.scalar.dma_start(out=notional_raw[:], in_=notional.rearrange("(g p t) -> p g t", p=P, t=PACK))
         nc.scalar.dma_start(out=fee_rows[:], in_=fee.rearrange("(p b) -> p b", p=P))
-        nc.scalar.dma_start(out=claim_cols[:], in_=claim.rearrange("(g p t) -> p g t", p=P, t=PACK))
+        nc.scalar.dma_start(out=claim_raw[:], in_=claim.rearrange("(g p t) -> p g t", p=P, t=PACK))
 
-        cash_raw = {}
-        disc_raw = {}
+        cash_raw, disc_raw = {}, {}
 
-        def load_cash(g, t):
-            raw = keep.tile([P, DATES], BF16, name="cash_raw_%d_%d" % (g, t))
+        def load_cash(tile):
+            g, t = divmod(tile, PACK)
+            cash_raw[tile] = keep.tile([P, DATES], BF16, name="cash_raw_%d" % tile)
             rows = cash[g * SPAN:(g + 1) * SPAN, :].rearrange("(p t) k -> p t k", t=PACK)
-            nc.sync.dma_start(out=raw[:], in_=rows[:, t, :])
-            cash_raw[g, t] = raw
+            nc.sync.dma_start(out=cash_raw[tile][:], in_=rows[:, t, :])
 
         def load_disc(c, h):
-            raw = keep.tile([P, PACK, HALF], BF16, name="disc_raw_%d_%d" % (c, h))
+            disc_raw[c, h] = keep.tile([P, PACK, HALF], BF16, name="disc_raw_%d_%d" % (c, h))
             rows = discount[c * SPAN:(c + 1) * SPAN, h * HALF:(h + 1) * HALF]
-            nc.sync.dma_start(out=raw[:], in_=rows.rearrange("(p j) n -> p j n", j=PACK))
-            disc_raw[c, h] = raw
+            nc.sync.dma_start(out=disc_raw[c, h][:], in_=rows.rearrange("(p j) n -> p j n", j=PACK))
 
-        for name in LOADS.split():
-            if name[0] == "D":
-                c = int(name[1])
-                raw = keep.tile([P, PACK, PATHS], BF16, name="disc_full_%d" % c)
-                nc.sync.dma_start(out=raw[:], in_=discount[c * SPAN:(c + 1) * SPAN, :].rearrange("(p j) n -> p j n", j=PACK))
-                for h in range(HALVES):
-                    disc_raw[c, h] = raw[:, :, h * HALF:(h + 1) * HALF]
-            elif name[0] == "d":
-                load_disc(int(name[1]), int(name[2]))
-            else:
-                load_cash(int(name[1]), int(name[2]))
+        for c in range(PASSES):
+            load_disc(c, 0)
+            load_cash(c)
+        load_cash(PACK - 1)
+        for c in range(PASSES):
+            load_disc(c, 1)
+        for tile in range(PACK, TILES - PACK):
+            load_cash(tile)
 
         ident = keep.tile([P, P], F32, name="ident")
         make_identity(nc, ident[:])
 
-        notional_cols = keep.tile([P, GROUPS * PACK], F32, name="notional_cols")
+        notional_cols = keep.tile([P, TILES], F32, name="notional_cols")
         nc.scalar.activation(out=notional_cols[:], in_=notional_raw[:].rearrange("p g t -> p (g t)"), func=ACT.Copy)
 
-        claim_flat = claim_cols[:].rearrange("p g t -> p (g t)")
-        at_claim = keep.tile([P, GROUPS * PACK], F32, name="at_claim")
-        at_floor = keep.tile([P, GROUPS * PACK], F32, name="at_floor")
-        lower = keep.tile([P, GROUPS * PACK], F32, name="lower")
-        upper = keep.tile([P, GROUPS * PACK], F32, name="upper")
+        lower = keep.tile([P, TILES], F32, name="lower")
+        upper = keep.tile([P, TILES], F32, name="upper")
 
-        def bounds():
-            nc.vector.tensor_tensor(out=at_claim[:], in0=claim_flat, in1=notional_cols[:], op=ALU.mult)
-            nc.vector.scalar_tensor_tensor(out=at_floor[:], in0=claim_flat, scalar=0.0, in1=notional_cols[:],
+        def make_bounds():
+            claim_cols = claim_raw[:].rearrange("p g t -> p (g t)")
+            at_claim = keep.tile([P, TILES], F32, name="at_claim")
+            at_floor = keep.tile([P, TILES], F32, name="at_floor")
+            nc.vector.tensor_tensor(out=at_claim[:], in0=claim_cols, in1=notional_cols[:], op=ALU.mult)
+            nc.vector.scalar_tensor_tensor(out=at_floor[:], in0=claim_cols, scalar=0.0, in1=notional_cols[:],
                                            op0=ALU.min, op1=ALU.mult)
             nc.vector.tensor_tensor(out=lower[:], in0=at_claim[:], in1=at_floor[:], op=ALU.min)
             nc.vector.tensor_tensor(out=upper[:], in0=at_claim[:], in1=at_floor[:], op=ALU.max)
 
         fee_all = keep.tile([P, PATHS], BF16, name="fee_all")
-        fee_bank = psum.tile([P, PACK, P], F32, name="fee_bank", tag="turned", bufs=RUN)
+        fee_bank = psum.tile([P, PACK, P], F32, name="fee_bank", tag="turned", bufs=TURN_BANKS)
         fee_words = fee_rows[:].bitcast(F32)
         for w in range(PACK):
             nc.tensor.transpose(fee_bank[:, w, :], fee_words[:, w:w + 1].to_broadcast([P, P]), ident[:])
@@ -115,215 +103,205 @@ def tile_senior_tranche_values_g2_kernel(tc, cash, discount, fee, claim, notiona
             nc.scalar.copy(out=fee_all[:].bitcast(F32).rearrange("p (n w) -> p n w", w=PACK),
                            in_=fee_bank[:].rearrange("p w n -> p n w"))
 
-        def interleave(dst, src, split, part="sv"):
-            width = src.shape[2]
-            for engine_copy, lo, hi, who in ((nc.vector.tensor_copy, 0, split, "v"), (nc.scalar.copy, split, width, "s")):
-                if hi > lo and who in part:
-                    engine_copy(out=dst[:, lo:hi, :].rearrange("p (c i) t -> p c t i", i=4),
-                                in_=src[:, :, lo:hi].rearrange("p t (c i) -> p c t i", i=4))
+        def interleave(copy, dst, src, lo, hi):
+            copy(out=dst[:, lo:hi, :].rearrange("p (c i) t -> p c t i", i=RUN),
+                 in_=src[:, :, lo:hi].rearrange("p t (c i) -> p c t i", i=RUN))
 
         disc_grouped, disc_codes, disc_scales = {}, {}, {}
 
-        def group_disc(c, h, split):
-            grouped = work.tile([P, HALF, PACK], BF16, name="disc_grouped", align_bytes=64)
-            interleave(grouped, disc_raw[c, h], split)
-            disc_grouped[c, h] = grouped
+        def group_disc(c, h, share):
+            disc_grouped[c, h] = work.tile([P, HALF, PACK], BF16, name="disc_grouped", align_bytes=64)
+            interleave(nc.vector.tensor_copy, disc_grouped[c, h], disc_raw[c, h], 0, share)
+            if share < HALF:
+                interleave(nc.scalar.copy, disc_grouped[c, h], disc_raw[c, h], share, HALF)
 
         def quantise_disc(c, h):
-            codes = keep.tile([P, HALF], U32, name="disc_codes_%d_%d" % (c, h), align_bytes=64)
-            scales = keep.tile([P, HALF], U8, name="disc_scales_%d_%d" % (c, h), align_bytes=64)
-            nc.vector.quantize_mx(out=codes[:].bitcast(FP8X4), scales=scales[:],
+            disc_codes[c, h] = keep.tile([P, HALF], U32, name="disc_codes_%d_%d" % (c, h), align_bytes=64)
+            disc_scales[c, h] = keep.tile([P, HALF], U8, name="disc_scales_%d_%d" % (c, h), align_bytes=64)
+            nc.vector.quantize_mx(out=disc_codes[c, h][:].bitcast(FP8X4), scales=disc_scales[c, h][:],
                                   in_=disc_grouped[c, h][:].rearrange("p n t -> p (n t)"))
-            disc_codes[c, h], disc_scales[c, h] = codes, scales
 
         turned, cash_grouped, cash_codes, cash_scales = {}, {}, {}, {}
-        banks = []
-        for j in range(0, SINGLE_TILES * PASSES, PASSES):
-            banks.extend([(j, j + 1), (j + 2,)])
-        banks.extend((j, j + 1) for j in range(SINGLE_TILES * PASSES, GROUPS * PACK * PASSES, 2))
-        place = {j: (b, s) for b, held in enumerate(banks) for s, j in enumerate(held)}
 
-        def turn_cash(b):
-            bank = psum.tile([P, len(banks[b]), 2, P], F32, name="turned", tag="turned", bufs=RUN)
-            for s, j in enumerate(banks[b]):
-                tile_no, c = divmod(j, PASSES)
-                words = cash_raw[divmod(tile_no, PACK)][:].bitcast(F32)
-                for u in range(2):
-                    nc.tensor.transpose(bank[:, s, u, :], words[:, 256 * c + u:256 * (c + 1):2], ident[:])
-            turned[b] = bank
+        def turn_cash(first, count):
+            blocks = [(tile, c) for tile in range(first, first + count) for c in range(PASSES)]
+            turned[first] = []
+            for b in range(0, len(blocks), 2):
+                bank = psum.tile([P, len(blocks[b:b + 2]), 2, P], F32, name="turned", tag="turned", bufs=TURN_BANKS)
+                for s, (tile, c) in enumerate(blocks[b:b + 2]):
+                    words = cash_raw[tile][:].bitcast(F32)
+                    for u in range(2):
+                        nc.tensor.transpose(bank[:, s, u, :], words[:, 256 * c + u:256 * (c + 1):2], ident[:])
+                turned[first].append(bank)
+            cash_grouped[first] = work.tile([P, len(blocks) * SPAN], BF16, name="cash_grouped", bufs=2, align_bytes=64)
+            codes = keep.tile([P, len(blocks) * P], U32, name="cash_codes_%d" % first, align_bytes=64)
+            scales = keep.tile([P, len(blocks) * P], U8, name="cash_scales_%d" % first, align_bytes=64)
+            cash_codes[first], cash_scales[first] = codes, scales
+            for b, (tile, c) in enumerate(blocks):
+                stationary[tile, c] = (codes[:, b * P:(b + 1) * P], scales[:, b * P:(b + 1) * P])
 
-        def group_cash(b, engine_copy):
-            grouped = work.tile([P, len(banks[b]) * SPAN], BF16, name="cash_grouped", bufs=6, align_bytes=64)
-            engine_copy(out=grouped[:].bitcast(F32).rearrange("p (s r u) -> p s r u", r=P, u=2),
-                        in_=turned[b][:].rearrange("p s u r -> p s r u"))
-            cash_grouped[b] = grouped
+        stationary = {}
 
-        def quantise_cash(b):
-            codes = keep.tile([P, len(banks[b]) * P], U32, name="cash_codes_%d" % b, align_bytes=64)
-            scales = keep.tile([P, len(banks[b]) * P], U8, name="cash_scales_%d" % b, align_bytes=64)
-            nc.vector.quantize_mx(out=codes[:].bitcast(FP8X4), scales=scales[:], in_=cash_grouped[b][:])
-            cash_codes[b], cash_scales[b] = codes, scales
+        def group_cash(first, banks):
+            for b in banks:
+                bank = turned[first][b]
+                cols = slice(2 * b * SPAN, (2 * b + bank.shape[1]) * SPAN)
+                nc.scalar.copy(out=cash_grouped[first][:, cols].bitcast(F32).rearrange("p (s r u) -> p s r u", r=P, u=2),
+                               in_=bank[:].rearrange("p s u r -> p s r u"))
 
-        units = UNITS
-        steps = [(g, h, t) for g, h in units for t in range(PACK)]
-        value, net, capped, y_tiles, y_grouped = {}, {}, {}, {}, {}
+        def quantise_cash(first, lo, hi):
+            nc.vector.quantize_mx(out=cash_codes[first][:, lo * P:hi * P].bitcast(FP8X4),
+                                  scales=cash_scales[first][:, lo * P:hi * P],
+                                  in_=cash_grouped[first][:, lo * SPAN:hi * SPAN])
+
+        fee_due, value, net, y, y_grouped = {}, {}, {}, {}, {}
         y_scales = keep.tile([P, PATHS], U8, name="y_scales", align_bytes=64)
 
-        def multiply(i):
-            g, h, t = steps[i]
-            acc = psum.tile([P, HALF], F32, name="acc", tag="acc", bufs=8 - RUN)
-            for c in range(PASSES):
-                b, s = place[(g * PACK + t) * PASSES + c]
-                cols = slice(s * P, (s + 1) * P)
-                nc.tensor.matmul_mx(out=acc[:], lhsT=cash_codes[b][:, cols].bitcast(FP8X4),
-                                    lhsT_scale=cash_scales[b][:, cols], rhs=disc_codes[c, h][:].bitcast(FP8X4),
-                                    rhs_scale=disc_scales[c, h][:], start=(c == 0), stop=(c == PASSES - 1))
-            value[i] = acc
-
-        fee_due = {}
-
-        def scale_fee(i, on_vector):
-            g, h, t = steps[i]
-            fee_due[i] = work.tile([P, HALF], F32, name="fee_due", bufs=FEE_BUFS)
+        def scale_fee(on_vector=False):
+            unit, t = divmod(len(fee_due), PACK)
+            g, h = divmod(unit, HALVES)
+            fee_due[unit, t] = work.tile([P, HALF], F32, name="fee_due", bufs=FEE_TILES)
             column = notional_cols[:, g * PACK + t:g * PACK + t + 1]
             fees = fee_all[:, h * HALF:(h + 1) * HALF]
             if on_vector:
-                nc.vector.tensor_scalar(out=fee_due[i][:], in0=fees, scalar1=column, scalar2=None, op0=ALU.mult)
+                nc.vector.tensor_scalar(out=fee_due[unit, t][:], in0=fees, scalar1=column, scalar2=None, op0=ALU.mult)
             else:
-                nc.scalar.activation(out=fee_due[i][:], in_=fees, func=ACT.Copy, scale=column)
+                nc.scalar.activation(out=fee_due[unit, t][:], in_=fees, func=ACT.Copy, scale=column)
 
-        def subtract_fee(i):
-            g, h, t = steps[i]
-            net[i] = work.tile([P, HALF], F32, name="net", bufs=5)
-            nc.vector.scalar_tensor_tensor(out=net[i][:], in0=value[i][:],
-                                           scalar=notional_cols[:, g * PACK + t:g * PACK + t + 1],
-                                           in1=fee_due[i][:], op0=ALU.mult, op1=ALU.subtract)
+        def multiply(unit, t):
+            g, h = divmod(unit, HALVES)
+            value[unit, t] = psum.tile([P, HALF], F32, name="value", tag="value", bufs=SUM_BANKS)
+            for c in range(PASSES):
+                codes, scales = stationary[g * PACK + t, c]
+                nc.tensor.matmul_mx(out=value[unit, t][:], lhsT=codes.bitcast(FP8X4), lhsT_scale=scales,
+                                    rhs=disc_codes[c, h][:].bitcast(FP8X4), rhs_scale=disc_scales[c, h][:],
+                                    start=(c == 0), stop=(c == PASSES - 1))
 
-        def cap(i, on_gpsimd=False):
-            g, h, t = steps[i]
+        def subtract_fee(unit, t):
+            g, h = divmod(unit, HALVES)
+            tile = g * PACK + t
+            net[unit, t] = work.tile([P, HALF], F32, name="net", bufs=2 * PACK)
+            nc.vector.scalar_tensor_tensor(out=net[unit, t][:], in0=value[unit, t][:],
+                                           scalar=notional_cols[:, tile:tile + 1],
+                                           in1=fee_due[unit, t][:],
+                                           op0=ALU.mult, op1=ALU.subtract)
+
+        def clamp(unit, t, engine):
+            g, h = divmod(unit, HALVES)
+            tile = g * PACK + t
             if t == 0:
-                y_tiles[g, h] = work.tile([P, PACK, HALF], F32, name="y")
-            j = g * PACK + t
-            engine = nc.gpsimd if on_gpsimd else nc.vector
-            engine.tensor_scalar(out=y_tiles[g, h][:, t, :], in0=net[i][:], scalar1=upper[:, j:j + 1],
-                                 scalar2=lower[:, j:j + 1], op0=ALU.min, op1=ALU.max)
-            nc.sync.dma_start(out=out_rows(g, h)[:, t, :], in_=y_tiles[g, h][:, t, :])
+                y[unit] = work.tile([P, PACK, HALF], F32, name="y")
+            engine.tensor_scalar(out=y[unit][:, t, :], in0=net[unit, t][:], scalar1=upper[:, tile:tile + 1],
+                                 scalar2=lower[:, tile:tile + 1], op0=ALU.min, op1=ALU.max)
+            rows = out_0[g * SPAN:(g + 1) * SPAN, h * HALF:(h + 1) * HALF].rearrange("(p t) m -> p t m", t=PACK)
+            nc.sync.dma_start(out=rows[:, t, :], in_=y[unit][:, t, :])
 
-        def out_rows(g, h):
-            return out_0[g * SPAN:(g + 1) * SPAN, h * HALF:(h + 1) * HALF].rearrange("(p t) m -> p t m", t=PACK)
+        def group_y(unit, share):
+            y_grouped[unit] = work.tile([P, HALF, PACK], BF16, name="y_grouped", bufs=2, align_bytes=64)
+            interleave(nc.scalar.copy, y_grouped[unit], y[unit], share, HALF)
 
-        def group_y(g, h, split, part):
-            if "s" in part:
-                y_grouped[g, h] = work.tile([P, HALF, PACK], BF16, name="y_grouped", bufs=2, align_bytes=64)
-            interleave(y_grouped[g, h], y_tiles[g, h], split, part)
-
-        def quantise_y(g, h):
-            cols = slice(h * HALF, (h + 1) * HALF)
-            codes = work.tile([P, HALF], U32, name="y_codes", align_bytes=64)
+        def quantise_y(unit, lo, hi):
+            g, h = divmod(unit, HALVES)
+            cols = slice(h * HALF + lo, h * HALF + hi)
+            codes = work.tile([P, hi - lo], U32, name="y_codes", align_bytes=64)
             nc.vector.quantize_mx(out=codes[:].bitcast(FP8X4), scales=y_scales[PACK * g:P, cols],
-                                  in_=y_grouped[g, h][:].rearrange("p n t -> p (n t)"))
+                                  in_=y_grouped[unit][:, lo:hi, :].rearrange("p n t -> p (n t)"))
             words = out_1[g].rearrange("p m t -> p (m t)").bitcast(I32)
             nc.sync.dma_start(out=words[:, cols], in_=codes[:].bitcast(I32))
 
-        def turn_run(first, end):
-            for b in range(first, end):
-                turn_cash(b)
-
-        def copy_run(first, end):
-            for b in range(first, end):
-                group_cash(b, nc.scalar.copy)
-
-        def quantise_run(first, end):
-            for b in range(first, end):
-                quantise_cash(b)
-
-        group_disc(0, 0, HEAD_SPLIT)
+        group_disc(0, 0, HEAD_SHARE)
         spread_fee()
-        turn_run(0, 2)
-        bounds()
+        turn_cash(0, 1)
+        make_bounds()
         quantise_disc(0, 0)
-        scale_fee(0, True)
-        scale_fee(1, True)
-        scale_fee(2, False)
-        copy_run(0, 1)
-        group_disc(1, 0, HEAD_SPLIT)
-        copy_run(1, 2)
-        quantise_cash(0)
+        scale_fee(on_vector=True)
+        group_disc(1, 0, HEAD_SHARE)
+        group_cash(0, [0, 1])
+        scale_fee(on_vector=True)
         quantise_disc(1, 0)
-        quantise_cash(1)
-        scale_fee(3, False)
-        turn_run(2, 4)
-        group_disc(2, 0, HEAD_SPLIT)
-        copy_run(2, 4)
-        scale_fee(4, True)
+        quantise_cash(0, 0, 2)
+        turn_cash(1, 1)
+        group_disc(2, 0, HEAD_SHARE)
+        group_cash(1, [0, 1])
+        quantise_cash(0, 2, 3)
         quantise_disc(2, 0)
-        quantise_run(2, 4)
-        scale_fee(5, True)
-        scale_fee(6, False)
-        scale_fee(7, False)
-        scale_fee(8, False)
-        multiply(0)
-        turn_run(4, 6)
-        copy_run(4, 6)
-        subtract_fee(0)
-        multiply(1)
-        turn_run(6, 8)
-        group_disc(0, 1, FIRST_SPLIT)
-        quantise_run(4, 6)
-        scale_fee(9, False)
-        copy_run(6, 8)
+        quantise_cash(1, 0, 2)
+        quantise_cash(1, 2, 3)
+        scale_fee(on_vector=True)
+        scale_fee(on_vector=True)
+        scale_fee()
+        scale_fee()
+        multiply(0, 0)
+        turn_cash(2, 1)
+        group_disc(0, 1, NEXT_SHARE)
+        group_cash(2, [0, 1])
+        subtract_fee(0, 0)
+        multiply(0, 1)
+        turn_cash(3, 1)
         quantise_disc(0, 1)
-        subtract_fee(1)
-        multiply(2)
-        quantise_run(6, 8)
-        group_disc(1, 1, NEXT_SPLIT)
-        multiply(3)
-        cap(0)
+        quantise_cash(2, 0, 2)
+        quantise_cash(2, 2, 3)
+        group_disc(1, 1, NEXT_SHARE)
+        group_cash(3, [0, 1])
+        subtract_fee(0, 1)
         quantise_disc(1, 1)
-        group_disc(2, 1, NEXT_SPLIT)
-        subtract_fee(2)
-        scale_fee(10, False)
+        multiply(0, 2)
+        quantise_cash(3, 0, 2)
+        quantise_cash(3, 2, 3)
+        group_disc(2, 1, NEXT_SHARE)
+        turn_cash(4, 2)
+        multiply(0, 3)
+        clamp(0, 0, nc.vector)
         quantise_disc(2, 1)
-        turn_run(8, 11)
-        copy_run(8, 11)
-        scale_fee(11, False)
-        cap(1)
-        subtract_fee(3)
-        cap(2)
-        cap(3)
-        for t in range(PACK):
-            load_cash(GROUPS - 1, t)
-        quantise_run(8, 11)
+        group_cash(4, range(TURN_BANKS))
+        scale_fee()
+        subtract_fee(0, 2)
+        clamp(0, 1, nc.vector)
+        subtract_fee(0, 3)
+        clamp(0, 2, nc.vector)
+        clamp(0, 3, nc.vector)
+        scale_fee()
+        scale_fee()
+        for tile in range(TILES - PACK, TILES):
+            load_cash(tile)
+        quantise_cash(4, 0, 4)
+        quantise_cash(4, 4, 6)
 
-        last = len(steps) - 1
-        for u in range(1, len(units)):
-            first = 11 + RUN * (u - 1)
-            turning = first < len(banks)
+        for unit in range(1, UNITS):
+            first = PACK + 2 * unit
+            turning = first < TILES
             for t in range(PACK):
                 if t == 1 and turning:
-                    turn_run(first, first + RUN)
-                multiply(PACK * u + t)
-                subtract_fee(PACK * u + t)
+                    turn_cash(first, 2)
+                multiply(unit, t)
+                subtract_fee(unit, t)
             for t in range(PACK):
-                cap(PACK * u + t, t < ON_GPSIMD and u >= G_FROM)
-            if u == 1:
-                copy_run(first, first + RUN)
-            group_y(units[u - 1][0], units[u - 1][1], OUT_SPLITS[u - 1], "s")
-            if turning and u > 1:
-                copy_run(first, first + RUN)
-            for j in range(len(fee_due), min(len(fee_due) + FEES[u - 1], last + 1)):
-                scale_fee(j, False)
-            group_y(units[u - 1][0], units[u - 1][1], OUT_SPLITS[u - 1], "v")
+                clamp(unit, t, nc.gpsimd if t < ON_GPSIMD else nc.vector)
+            share = OUT_SHARE if turning else 0
+            if unit == 1:
+                group_cash(first, range(TURN_BANKS))
+            group_y(unit - 1, share)
+            if turning and unit > 1:
+                group_cash(first, range(TURN_BANKS))
+            for j in range(FEES[unit - 1]):
+                scale_fee()
             if turning:
-                quantise_run(first, first + 1)
-            quantise_y(*units[u - 1])
+                interleave(nc.vector.tensor_copy, y_grouped[unit - 1], y[unit - 1], 0, share)
+                quantise_cash(first, 0, 4)
+            if unit < UNITS - 1:
+                quantise_y(unit - 1, 0, HALF)
             if turning:
-                quantise_run(first + 1, first + RUN)
-        group_y(units[-1][0], units[-1][1], OUT_SPLITS[-1], "sv")
-        quantise_y(*units[-1])
+                quantise_cash(first, 4, 6)
+
+        last = UNITS - 1
+        group_y(last, LAST_SHARE)
+        interleave(nc.vector.tensor_copy, y_grouped[last], y[last], 0, LAST_SHARE)
+        quantise_y(last - 1, 0, HALF)
+        quantise_y(last, 0, LAST_SHARE)
+        quantise_y(last, LAST_SHARE, HALF)
 
         scale_rows = out_2.bitcast(I32)
         for q in range(4):
             queue = nc.scalar if q < 2 else nc.sync
             queue.dma_start(out=scale_rows[:, 4 * q:4 * q + 4, :],
-                              in_=y_scales[32 * q:32 * q + 4 * GROUPS, :].bitcast(I32))
+                            in_=y_scales[32 * q:32 * q + 4 * GROUPS, :].bitcast(I32))

@@ -26,22 +26,23 @@ HALVES = PATHS // HALF
 UNITS = GROUPS * HALVES
 TURN_BANKS = 3
 SUM_BANKS = 8 - TURN_BANKS
-RUN = 4
+NEIGHBOURS = 4
 
-HEAD_SHARE = 320
-NEXT_SHARE = 320
+QUADRANT = 32
+
+DISC_SHARE = 320
 OUT_SHARE = 224
-LAST_SHARE = 256
+LAST_SHARE = HALF // 2
 ON_GPSIMD = 2
-FEE_TILES = 14
-FEES = (4, 4, 4, 4, 4, 3, 0)
+FEE_TILES = 3 * PACK
+CASH_TILES = 2 * PACK
 
 
 def tile_senior_tranche_values_g2_kernel(tc, cash, discount, fee, claim, notional, out_0, out_1, out_2):
     nc = tc.nc
     with ExitStack() as ctx:
         keep = ctx.enter_context(tc.tile_pool(name="keep", bufs=1))
-        work = ctx.enter_context(tc.tile_pool(name="work", bufs=3))
+        work = ctx.enter_context(tc.tile_pool(name="work", bufs=2))
         psum = ctx.enter_context(tc.psum_pool(name="psum", bufs=1))
         ctx.enter_context(tc.manual_schedule())
 
@@ -56,12 +57,13 @@ def tile_senior_tranche_values_g2_kernel(tc, cash, discount, fee, claim, notiona
 
         def load_cash(tile):
             g, t = divmod(tile, PACK)
-            cash_raw[tile] = keep.tile([P, DATES], BF16, name="cash_raw_%d" % tile)
+            cash_raw[tile] = work.tile([P, DATES], BF16, name="cash_raw", bufs=CASH_TILES)
             rows = cash[g * SPAN:(g + 1) * SPAN, :].rearrange("(p t) k -> p t k", t=PACK)
             nc.sync.dma_start(out=cash_raw[tile][:], in_=rows[:, t, :])
 
         def load_disc(c, h):
-            disc_raw[c, h] = keep.tile([P, PACK, HALF], BF16, name="disc_raw_%d_%d" % (c, h))
+            disc_raw[c, h] = work.tile([P, PACK, HALF], BF16, name="disc_raw", tag="staged", bufs=UNITS,
+                                       align_bytes=64)
             rows = discount[c * SPAN:(c + 1) * SPAN, h * HALF:(h + 1) * HALF]
             nc.sync.dma_start(out=disc_raw[c, h][:], in_=rows.rearrange("(p j) n -> p j n", j=PACK))
 
@@ -71,7 +73,7 @@ def tile_senior_tranche_values_g2_kernel(tc, cash, discount, fee, claim, notiona
         load_cash(PACK - 1)
         for c in range(PASSES):
             load_disc(c, 1)
-        for tile in range(PACK, TILES - PACK):
+        for tile in range(PACK, 2 * PACK):
             load_cash(tile)
 
         ident = keep.tile([P, P], F32, name="ident")
@@ -95,66 +97,62 @@ def tile_senior_tranche_values_g2_kernel(tc, cash, discount, fee, claim, notiona
 
         fee_all = keep.tile([P, PATHS], BF16, name="fee_all")
         fee_bank = psum.tile([P, PACK, P], F32, name="fee_bank", tag="turned", bufs=TURN_BANKS)
-        fee_words = fee_rows[:].bitcast(F32)
+        fee_pairs = fee_rows[:].bitcast(F32)
         for w in range(PACK):
-            nc.tensor.transpose(fee_bank[:, w, :], fee_words[:, w:w + 1].to_broadcast([P, P]), ident[:])
+            nc.tensor.transpose(fee_bank[:, w, :], fee_pairs[:, w:w + 1].to_broadcast([P, P]), ident[:])
 
         def spread_fee():
             nc.scalar.copy(out=fee_all[:].bitcast(F32).rearrange("p (n w) -> p n w", w=PACK),
                            in_=fee_bank[:].rearrange("p w n -> p n w"))
 
         def interleave(copy, dst, src, lo, hi):
-            copy(out=dst[:, lo:hi, :].rearrange("p (c i) t -> p c t i", i=RUN),
-                 in_=src[:, :, lo:hi].rearrange("p t (c i) -> p c t i", i=RUN))
+            copy(out=dst[:, lo:hi, :].rearrange("p (c i) t -> p c t i", i=NEIGHBOURS),
+                 in_=src[:, :, lo:hi].rearrange("p t (c i) -> p c t i", i=NEIGHBOURS))
 
-        disc_grouped, disc_codes, disc_scales = {}, {}, {}
+        disc_laid, disc_codes, disc_scales = {}, {}, {}
 
-        def group_disc(c, h, share):
-            disc_grouped[c, h] = work.tile([P, HALF, PACK], BF16, name="disc_grouped", align_bytes=64)
-            interleave(nc.vector.tensor_copy, disc_grouped[c, h], disc_raw[c, h], 0, share)
-            if share < HALF:
-                interleave(nc.scalar.copy, disc_grouped[c, h], disc_raw[c, h], share, HALF)
+        def lay_disc(c, h):
+            disc_laid[c, h] = work.tile([P, HALF, PACK], BF16, name="disc_laid", align_bytes=64)
+            interleave(nc.vector.tensor_copy, disc_laid[c, h], disc_raw[c, h], 0, DISC_SHARE)
+            interleave(nc.scalar.copy, disc_laid[c, h], disc_raw[c, h], DISC_SHARE, HALF)
 
         def quantise_disc(c, h):
             disc_codes[c, h] = keep.tile([P, HALF], U32, name="disc_codes_%d_%d" % (c, h), align_bytes=64)
             disc_scales[c, h] = keep.tile([P, HALF], U8, name="disc_scales_%d_%d" % (c, h), align_bytes=64)
             nc.vector.quantize_mx(out=disc_codes[c, h][:].bitcast(FP8X4), scales=disc_scales[c, h][:],
-                                  in_=disc_grouped[c, h][:].rearrange("p n t -> p (n t)"))
+                                  in_=disc_laid[c, h][:].rearrange("p n t -> p (n t)"))
 
-        turned, cash_grouped, cash_codes, cash_scales = {}, {}, {}, {}
+        turned, cash_laid, cash_codes, cash_scales, stationary = {}, {}, {}, {}, {}
 
         def turn_cash(first, count):
-            blocks = [(tile, c) for tile in range(first, first + count) for c in range(PASSES)]
+            panels = [(tile, c) for tile in range(first, first + count) for c in range(PASSES)]
             turned[first] = []
-            for b in range(0, len(blocks), 2):
-                bank = psum.tile([P, len(blocks[b:b + 2]), 2, P], F32, name="turned", tag="turned", bufs=TURN_BANKS)
-                for s, (tile, c) in enumerate(blocks[b:b + 2]):
-                    words = cash_raw[tile][:].bitcast(F32)
+            for b in range(0, len(panels), 2):
+                bank = psum.tile([P, len(panels[b:b + 2]), 2, P], F32, name="turned", tag="turned", bufs=TURN_BANKS)
+                for s, (tile, c) in enumerate(panels[b:b + 2]):
+                    pairs = cash_raw[tile][:].bitcast(F32)
                     for u in range(2):
-                        nc.tensor.transpose(bank[:, s, u, :], words[:, 256 * c + u:256 * (c + 1):2], ident[:])
+                        nc.tensor.transpose(bank[:, s, u, :], pairs[:, 2 * P * c + u:2 * P * (c + 1):2], ident[:])
                 turned[first].append(bank)
-            cash_grouped[first] = work.tile([P, len(blocks) * SPAN], BF16, name="cash_grouped", bufs=2, align_bytes=64)
-            codes = keep.tile([P, len(blocks) * P], U32, name="cash_codes_%d" % first, align_bytes=64)
-            scales = keep.tile([P, len(blocks) * P], U8, name="cash_scales_%d" % first, align_bytes=64)
+            cash_laid[first] = work.tile([P, len(panels) * SPAN], BF16, name="cash_laid", align_bytes=64)
+            codes = keep.tile([P, len(panels) * P], U32, name="cash_codes_%d" % first, align_bytes=64)
+            scales = keep.tile([P, len(panels) * P], U8, name="cash_scales_%d" % first, align_bytes=64)
             cash_codes[first], cash_scales[first] = codes, scales
-            for b, (tile, c) in enumerate(blocks):
+            for b, (tile, c) in enumerate(panels):
                 stationary[tile, c] = (codes[:, b * P:(b + 1) * P], scales[:, b * P:(b + 1) * P])
 
-        stationary = {}
-
-        def group_cash(first, banks):
-            for b in banks:
-                bank = turned[first][b]
-                cols = slice(2 * b * SPAN, (2 * b + bank.shape[1]) * SPAN)
-                nc.scalar.copy(out=cash_grouped[first][:, cols].bitcast(F32).rearrange("p (s r u) -> p s r u", r=P, u=2),
+        def lay_cash(first):
+            for b, bank in enumerate(turned[first]):
+                pairs = cash_laid[first][:, 2 * b * SPAN:(2 * b + bank.shape[1]) * SPAN].bitcast(F32)
+                nc.scalar.copy(out=pairs.rearrange("p (s r u) -> p s r u", r=P, u=2),
                                in_=bank[:].rearrange("p s u r -> p s r u"))
 
         def quantise_cash(first, lo, hi):
             nc.vector.quantize_mx(out=cash_codes[first][:, lo * P:hi * P].bitcast(FP8X4),
                                   scales=cash_scales[first][:, lo * P:hi * P],
-                                  in_=cash_grouped[first][:, lo * SPAN:hi * SPAN])
+                                  in_=cash_laid[first][:, lo * SPAN:hi * SPAN])
 
-        fee_due, value, net, y, y_grouped = {}, {}, {}, {}, {}
+        fee_due, value, net, y, y_laid = {}, {}, {}, {}, {}
         y_scales = keep.tile([P, PATHS], U8, name="y_scales", align_bytes=64)
 
         def scale_fee(on_vector=False):
@@ -182,47 +180,47 @@ def tile_senior_tranche_values_g2_kernel(tc, cash, discount, fee, claim, notiona
             tile = g * PACK + t
             net[unit, t] = work.tile([P, HALF], F32, name="net", bufs=2 * PACK)
             nc.vector.scalar_tensor_tensor(out=net[unit, t][:], in0=value[unit, t][:],
-                                           scalar=notional_cols[:, tile:tile + 1],
-                                           in1=fee_due[unit, t][:],
+                                           scalar=notional_cols[:, tile:tile + 1], in1=fee_due[unit, t][:],
                                            op0=ALU.mult, op1=ALU.subtract)
 
         def clamp(unit, t, engine):
             g, h = divmod(unit, HALVES)
             tile = g * PACK + t
             if t == 0:
-                y[unit] = work.tile([P, PACK, HALF], F32, name="y")
+                y[unit] = keep.tile([P, PACK, HALF], F32, name="y_%d" % unit)
             engine.tensor_scalar(out=y[unit][:, t, :], in0=net[unit, t][:], scalar1=upper[:, tile:tile + 1],
                                  scalar2=lower[:, tile:tile + 1], op0=ALU.min, op1=ALU.max)
             rows = out_0[g * SPAN:(g + 1) * SPAN, h * HALF:(h + 1) * HALF].rearrange("(p t) m -> p t m", t=PACK)
             nc.sync.dma_start(out=rows[:, t, :], in_=y[unit][:, t, :])
 
-        def group_y(unit, share):
-            y_grouped[unit] = work.tile([P, HALF, PACK], BF16, name="y_grouped", bufs=2, align_bytes=64)
-            interleave(nc.scalar.copy, y_grouped[unit], y[unit], share, HALF)
+        def lay_y(unit, share):
+            y_laid[unit] = work.tile([P, HALF, PACK], BF16, name="y_laid", align_bytes=64)
+            interleave(nc.scalar.copy, y_laid[unit], y[unit], share, HALF)
 
         def quantise_y(unit, lo, hi):
             g, h = divmod(unit, HALVES)
             cols = slice(h * HALF + lo, h * HALF + hi)
-            codes = work.tile([P, hi - lo], U32, name="y_codes", align_bytes=64)
+            codes = work.tile([P, hi - lo], U32, name="y_codes", tag="staged", bufs=UNITS, align_bytes=64)
             nc.vector.quantize_mx(out=codes[:].bitcast(FP8X4), scales=y_scales[PACK * g:P, cols],
-                                  in_=y_grouped[unit][:, lo:hi, :].rearrange("p n t -> p (n t)"))
+                                  in_=y_laid[unit][:, lo:hi, :].rearrange("p n t -> p (n t)"))
             words = out_1[g].rearrange("p m t -> p (m t)").bitcast(I32)
             nc.sync.dma_start(out=words[:, cols], in_=codes[:].bitcast(I32))
 
-        group_disc(0, 0, HEAD_SHARE)
+        lay_disc(0, 0)
         spread_fee()
         turn_cash(0, 1)
         make_bounds()
         quantise_disc(0, 0)
         scale_fee(on_vector=True)
-        group_disc(1, 0, HEAD_SHARE)
-        group_cash(0, [0, 1])
+        scale_fee()
+        lay_disc(1, 0)
+        lay_cash(0)
         scale_fee(on_vector=True)
         quantise_disc(1, 0)
         quantise_cash(0, 0, 2)
         turn_cash(1, 1)
-        group_disc(2, 0, HEAD_SHARE)
-        group_cash(1, [0, 1])
+        lay_disc(2, 0)
+        lay_cash(1)
         quantise_cash(0, 2, 3)
         quantise_disc(2, 0)
         quantise_cash(1, 0, 2)
@@ -231,41 +229,43 @@ def tile_senior_tranche_values_g2_kernel(tc, cash, discount, fee, claim, notiona
         scale_fee(on_vector=True)
         scale_fee()
         scale_fee()
+
         multiply(0, 0)
         turn_cash(2, 1)
-        group_disc(0, 1, NEXT_SHARE)
-        group_cash(2, [0, 1])
+        lay_disc(0, 1)
+        lay_cash(2)
         subtract_fee(0, 0)
         multiply(0, 1)
         turn_cash(3, 1)
+        for tile in range(2 * PACK, 3 * PACK):
+            load_cash(tile)
         quantise_disc(0, 1)
         quantise_cash(2, 0, 2)
         quantise_cash(2, 2, 3)
-        group_disc(1, 1, NEXT_SHARE)
-        group_cash(3, [0, 1])
+        lay_disc(1, 1)
+        lay_cash(3)
         subtract_fee(0, 1)
         quantise_disc(1, 1)
         multiply(0, 2)
         quantise_cash(3, 0, 2)
         quantise_cash(3, 2, 3)
-        group_disc(2, 1, NEXT_SHARE)
-        turn_cash(4, 2)
+        lay_disc(2, 1)
+
+        turn_cash(PACK, 2)
         multiply(0, 3)
         clamp(0, 0, nc.vector)
         quantise_disc(2, 1)
-        group_cash(4, range(TURN_BANKS))
+        lay_cash(PACK)
         scale_fee()
         subtract_fee(0, 2)
         clamp(0, 1, nc.vector)
         subtract_fee(0, 3)
         clamp(0, 2, nc.vector)
         clamp(0, 3, nc.vector)
-        scale_fee()
-        scale_fee()
-        for tile in range(TILES - PACK, TILES):
-            load_cash(tile)
-        quantise_cash(4, 0, 4)
-        quantise_cash(4, 4, 6)
+        for t in range(PACK):
+            scale_fee()
+        quantise_cash(PACK, 0, 4)
+        quantise_cash(PACK, 4, 6)
 
         for unit in range(1, UNITS):
             first = PACK + 2 * unit
@@ -273,35 +273,37 @@ def tile_senior_tranche_values_g2_kernel(tc, cash, discount, fee, claim, notiona
             for t in range(PACK):
                 if t == 1 and turning:
                     turn_cash(first, 2)
+                    if unit == 1:
+                        for tile in range(3 * PACK, TILES):
+                            load_cash(tile)
                 multiply(unit, t)
                 subtract_fee(unit, t)
+                if t == 0 and unit > 1:
+                    quantise_y(unit - 2, 0, HALF)
             for t in range(PACK):
                 clamp(unit, t, nc.gpsimd if t < ON_GPSIMD else nc.vector)
             share = OUT_SHARE if turning else 0
             if unit == 1:
-                group_cash(first, range(TURN_BANKS))
-            group_y(unit - 1, share)
-            if turning and unit > 1:
-                group_cash(first, range(TURN_BANKS))
-            for j in range(FEES[unit - 1]):
-                scale_fee()
+                lay_cash(first)
+            lay_y(unit - 1, share)
             if turning:
-                interleave(nc.vector.tensor_copy, y_grouped[unit - 1], y[unit - 1], 0, share)
+                if unit > 1:
+                    lay_cash(first)
+                for t in range(PACK):
+                    scale_fee()
+                interleave(nc.vector.tensor_copy, y_laid[unit - 1], y[unit - 1], 0, share)
                 quantise_cash(first, 0, 4)
-            if unit < UNITS - 1:
-                quantise_y(unit - 1, 0, HALF)
-            if turning:
                 quantise_cash(first, 4, 6)
 
         last = UNITS - 1
-        group_y(last, LAST_SHARE)
-        interleave(nc.vector.tensor_copy, y_grouped[last], y[last], 0, LAST_SHARE)
+        lay_y(last, LAST_SHARE)
+        interleave(nc.vector.tensor_copy, y_laid[last], y[last], 0, LAST_SHARE)
         quantise_y(last - 1, 0, HALF)
         quantise_y(last, 0, LAST_SHARE)
         quantise_y(last, LAST_SHARE, HALF)
 
         scale_rows = out_2.bitcast(I32)
-        for q in range(4):
+        for q in range(P // QUADRANT):
             queue = nc.scalar if q < 2 else nc.sync
-            queue.dma_start(out=scale_rows[:, 4 * q:4 * q + 4, :],
-                            in_=y_scales[32 * q:32 * q + 4 * GROUPS, :].bitcast(I32))
+            queue.dma_start(out=scale_rows[:, PACK * q:PACK * (q + 1), :],
+                            in_=y_scales[QUADRANT * q:QUADRANT * q + PACK * GROUPS, :].bitcast(I32))

from contextlib import ExitStack

import concourse.mybir as mybir
from concourse.masks import make_identity

POOLS, DATES, PATHS = 2048, 1536, 1024
FLOPS = 2 * POOLS * DATES * PATHS

F32 = mybir.dt.float32
BF16 = mybir.dt.bfloat16
I32 = mybir.dt.int32
U32 = mybir.dt.uint32
U8 = mybir.dt.uint8
FP8X4 = mybir.dt.float8_e4m3fn_x4
ALU = mybir.AluOpType
ACT = mybir.ActivationFunctionType

P = 128
PACK = 4
SPAN = P * PACK
PASSES = DATES // SPAN
GROUPS = POOLS // SPAN
TILES = GROUPS * PACK
HALF = 512
HALVES = PATHS // HALF
UNITS = GROUPS * HALVES
TURN_BANKS = 3
SUM_BANKS = 8 - TURN_BANKS
NEIGHBOURS = 4

QUADRANT = 32

DISC_SHARE = 320
OUT_SHARE = 224
LAST_SHARE = HALF // 2
ON_GPSIMD = 2
FEE_TILES = 3 * PACK
CASH_TILES = 2 * PACK


def tile_senior_tranche_values_g2_kernel(tc, cash, discount, fee, claim, notional, out_0, out_1, out_2):
    nc = tc.nc
    with ExitStack() as ctx:
        keep = ctx.enter_context(tc.tile_pool(name="keep", bufs=1))
        work = ctx.enter_context(tc.tile_pool(name="work", bufs=2))
        psum = ctx.enter_context(tc.psum_pool(name="psum", bufs=1))
        ctx.enter_context(tc.manual_schedule())

        notional_raw = keep.tile([P, GROUPS, PACK], BF16, name="notional_raw")
        fee_rows = keep.tile([P, PATHS // P], BF16, name="fee_rows")
        claim_raw = keep.tile([P, GROUPS, PACK], BF16, name="claim_raw")
        nc.scalar.dma_start(out=notional_raw[:], in_=notional.rearrange("(g p t) -> p g t", p=P, t=PACK))
        nc.scalar.dma_start(out=fee_rows[:], in_=fee.rearrange("(p b) -> p b", p=P))
        nc.scalar.dma_start(out=claim_raw[:], in_=claim.rearrange("(g p t) -> p g t", p=P, t=PACK))

        cash_raw, disc_raw = {}, {}

        def load_cash(tile):
            g, t = divmod(tile, PACK)
            cash_raw[tile] = work.tile([P, DATES], BF16, name="cash_raw", bufs=CASH_TILES)
            rows = cash[g * SPAN:(g + 1) * SPAN, :].rearrange("(p t) k -> p t k", t=PACK)
            nc.sync.dma_start(out=cash_raw[tile][:], in_=rows[:, t, :])

        def load_disc(c, h):
            disc_raw[c, h] = work.tile([P, PACK, HALF], BF16, name="disc_raw", tag="staged", bufs=UNITS,
                                       align_bytes=64)
            rows = discount[c * SPAN:(c + 1) * SPAN, h * HALF:(h + 1) * HALF]
            nc.sync.dma_start(out=disc_raw[c, h][:], in_=rows.rearrange("(p j) n -> p j n", j=PACK))

        for c in range(PASSES):
            load_disc(c, 0)
            load_cash(c)
        load_cash(PACK - 1)
        for c in range(PASSES):
            load_disc(c, 1)
        for tile in range(PACK, 2 * PACK):
            load_cash(tile)

        ident = keep.tile([P, P], F32, name="ident")
        make_identity(nc, ident[:])

        notional_cols = keep.tile([P, TILES], F32, name="notional_cols")
        nc.scalar.activation(out=notional_cols[:], in_=notional_raw[:].rearrange("p g t -> p (g t)"), func=ACT.Copy)

        lower = keep.tile([P, TILES], F32, name="lower")
        upper = keep.tile([P, TILES], F32, name="upper")

        def make_bounds():
            claim_cols = claim_raw[:].rearrange("p g t -> p (g t)")
            at_claim = keep.tile([P, TILES], F32, name="at_claim")
            at_floor = keep.tile([P, TILES], F32, name="at_floor")
            nc.vector.tensor_tensor(out=at_claim[:], in0=claim_cols, in1=notional_cols[:], op=ALU.mult)
            nc.vector.scalar_tensor_tensor(out=at_floor[:], in0=claim_cols, scalar=0.0, in1=notional_cols[:],
                                           op0=ALU.min, op1=ALU.mult)
            nc.vector.tensor_tensor(out=lower[:], in0=at_claim[:], in1=at_floor[:], op=ALU.min)
            nc.vector.tensor_tensor(out=upper[:], in0=at_claim[:], in1=at_floor[:], op=ALU.max)

        fee_all = keep.tile([P, PATHS], BF16, name="fee_all")
        fee_bank = psum.tile([P, PACK, P], F32, name="fee_bank", tag="turned", bufs=TURN_BANKS)
        fee_pairs = fee_rows[:].bitcast(F32)
        for w in range(PACK):
            nc.tensor.transpose(fee_bank[:, w, :], fee_pairs[:, w:w + 1].to_broadcast([P, P]), ident[:])

        def spread_fee():
            nc.scalar.copy(out=fee_all[:].bitcast(F32).rearrange("p (n w) -> p n w", w=PACK),
                           in_=fee_bank[:].rearrange("p w n -> p n w"))

        def interleave(copy, dst, src, lo, hi):
            copy(out=dst[:, lo:hi, :].rearrange("p (c i) t -> p c t i", i=NEIGHBOURS),
                 in_=src[:, :, lo:hi].rearrange("p t (c i) -> p c t i", i=NEIGHBOURS))

        disc_laid, disc_codes, disc_scales = {}, {}, {}

        def lay_disc(c, h):
            disc_laid[c, h] = work.tile([P, HALF, PACK], BF16, name="disc_laid", align_bytes=64)
            interleave(nc.vector.tensor_copy, disc_laid[c, h], disc_raw[c, h], 0, DISC_SHARE)
            interleave(nc.scalar.copy, disc_laid[c, h], disc_raw[c, h], DISC_SHARE, HALF)

        def quantise_disc(c, h):
            disc_codes[c, h] = keep.tile([P, HALF], U32, name="disc_codes_%d_%d" % (c, h), align_bytes=64)
            disc_scales[c, h] = keep.tile([P, HALF], U8, name="disc_scales_%d_%d" % (c, h), align_bytes=64)
            nc.vector.quantize_mx(out=disc_codes[c, h][:].bitcast(FP8X4), scales=disc_scales[c, h][:],
                                  in_=disc_laid[c, h][:].rearrange("p n t -> p (n t)"))

        turned, cash_laid, cash_codes, cash_scales, stationary = {}, {}, {}, {}, {}

        def turn_cash(first, count):
            panels = [(tile, c) for tile in range(first, first + count) for c in range(PASSES)]
            turned[first] = []
            for b in range(0, len(panels), 2):
                bank = psum.tile([P, len(panels[b:b + 2]), 2, P], F32, name="turned", tag="turned", bufs=TURN_BANKS)
                for s, (tile, c) in enumerate(panels[b:b + 2]):
                    pairs = cash_raw[tile][:].bitcast(F32)
                    for u in range(2):
                        nc.tensor.transpose(bank[:, s, u, :], pairs[:, 2 * P * c + u:2 * P * (c + 1):2], ident[:])
                turned[first].append(bank)
            cash_laid[first] = work.tile([P, len(panels) * SPAN], BF16, name="cash_laid", align_bytes=64)
            codes = keep.tile([P, len(panels) * P], U32, name="cash_codes_%d" % first, align_bytes=64)
            scales = keep.tile([P, len(panels) * P], U8, name="cash_scales_%d" % first, align_bytes=64)
            cash_codes[first], cash_scales[first] = codes, scales
            for b, (tile, c) in enumerate(panels):
                stationary[tile, c] = (codes[:, b * P:(b + 1) * P], scales[:, b * P:(b + 1) * P])

        def lay_cash(first):
            for b, bank in enumerate(turned[first]):
                pairs = cash_laid[first][:, 2 * b * SPAN:(2 * b + bank.shape[1]) * SPAN].bitcast(F32)
                nc.scalar.copy(out=pairs.rearrange("p (s r u) -> p s r u", r=P, u=2),
                               in_=bank[:].rearrange("p s u r -> p s r u"))

        def quantise_cash(first, lo, hi):
            nc.vector.quantize_mx(out=cash_codes[first][:, lo * P:hi * P].bitcast(FP8X4),
                                  scales=cash_scales[first][:, lo * P:hi * P],
                                  in_=cash_laid[first][:, lo * SPAN:hi * SPAN])

        fee_due, value, net, y, y_laid = {}, {}, {}, {}, {}
        y_scales = keep.tile([P, PATHS], U8, name="y_scales", align_bytes=64)

        def scale_fee(on_vector=False):
            unit, t = divmod(len(fee_due), PACK)
            g, h = divmod(unit, HALVES)
            fee_due[unit, t] = work.tile([P, HALF], F32, name="fee_due", bufs=FEE_TILES)
            column = notional_cols[:, g * PACK + t:g * PACK + t + 1]
            fees = fee_all[:, h * HALF:(h + 1) * HALF]
            if on_vector:
                nc.vector.tensor_scalar(out=fee_due[unit, t][:], in0=fees, scalar1=column, scalar2=None, op0=ALU.mult)
            else:
                nc.scalar.activation(out=fee_due[unit, t][:], in_=fees, func=ACT.Copy, scale=column)

        def multiply(unit, t):
            g, h = divmod(unit, HALVES)
            value[unit, t] = psum.tile([P, HALF], F32, name="value", tag="value", bufs=SUM_BANKS)
            for c in range(PASSES):
                codes, scales = stationary[g * PACK + t, c]
                nc.tensor.matmul_mx(out=value[unit, t][:], lhsT=codes.bitcast(FP8X4), lhsT_scale=scales,
                                    rhs=disc_codes[c, h][:].bitcast(FP8X4), rhs_scale=disc_scales[c, h][:],
                                    start=(c == 0), stop=(c == PASSES - 1))

        def subtract_fee(unit, t):
            g, h = divmod(unit, HALVES)
            tile = g * PACK + t
            net[unit, t] = work.tile([P, HALF], F32, name="net", bufs=2 * PACK)
            nc.vector.scalar_tensor_tensor(out=net[unit, t][:], in0=value[unit, t][:],
                                           scalar=notional_cols[:, tile:tile + 1], in1=fee_due[unit, t][:],
                                           op0=ALU.mult, op1=ALU.subtract)

        def clamp(unit, t, engine):
            g, h = divmod(unit, HALVES)
            tile = g * PACK + t
            if t == 0:
                y[unit] = keep.tile([P, PACK, HALF], F32, name="y_%d" % unit)
            engine.tensor_scalar(out=y[unit][:, t, :], in0=net[unit, t][:], scalar1=upper[:, tile:tile + 1],
                                 scalar2=lower[:, tile:tile + 1], op0=ALU.min, op1=ALU.max)
            rows = out_0[g * SPAN:(g + 1) * SPAN, h * HALF:(h + 1) * HALF].rearrange("(p t) m -> p t m", t=PACK)
            nc.sync.dma_start(out=rows[:, t, :], in_=y[unit][:, t, :])

        def lay_y(unit, share):
            y_laid[unit] = work.tile([P, HALF, PACK], BF16, name="y_laid", align_bytes=64)
            interleave(nc.scalar.copy, y_laid[unit], y[unit], share, HALF)

        def quantise_y(unit, lo, hi):
            g, h = divmod(unit, HALVES)
            cols = slice(h * HALF + lo, h * HALF + hi)
            codes = work.tile([P, hi - lo], U32, name="y_codes", tag="staged", bufs=UNITS, align_bytes=64)
            nc.vector.quantize_mx(out=codes[:].bitcast(FP8X4), scales=y_scales[PACK * g:P, cols],
                                  in_=y_laid[unit][:, lo:hi, :].rearrange("p n t -> p (n t)"))
            words = out_1[g].rearrange("p m t -> p (m t)").bitcast(I32)
            nc.sync.dma_start(out=words[:, cols], in_=codes[:].bitcast(I32))

        lay_disc(0, 0)
        spread_fee()
        turn_cash(0, 1)
        make_bounds()
        quantise_disc(0, 0)
        scale_fee(on_vector=True)
        scale_fee()
        lay_disc(1, 0)
        lay_cash(0)
        scale_fee(on_vector=True)
        quantise_disc(1, 0)
        quantise_cash(0, 0, 2)
        turn_cash(1, 1)
        lay_disc(2, 0)
        lay_cash(1)
        quantise_cash(0, 2, 3)
        quantise_disc(2, 0)
        quantise_cash(1, 0, 2)
        quantise_cash(1, 2, 3)
        scale_fee(on_vector=True)
        scale_fee(on_vector=True)
        scale_fee()
        scale_fee()

        multiply(0, 0)
        turn_cash(2, 1)
        lay_disc(0, 1)
        lay_cash(2)
        subtract_fee(0, 0)
        multiply(0, 1)
        turn_cash(3, 1)
        for tile in range(2 * PACK, 3 * PACK):
            load_cash(tile)
        quantise_disc(0, 1)
        quantise_cash(2, 0, 2)
        quantise_cash(2, 2, 3)
        lay_disc(1, 1)
        lay_cash(3)
        subtract_fee(0, 1)
        quantise_disc(1, 1)
        multiply(0, 2)
        quantise_cash(3, 0, 2)
        quantise_cash(3, 2, 3)
        lay_disc(2, 1)

        turn_cash(PACK, 2)
        multiply(0, 3)
        clamp(0, 0, nc.vector)
        quantise_disc(2, 1)
        lay_cash(PACK)
        scale_fee()
        subtract_fee(0, 2)
        clamp(0, 1, nc.vector)
        subtract_fee(0, 3)
        clamp(0, 2, nc.vector)
        clamp(0, 3, nc.vector)
        for t in range(PACK):
            scale_fee()
        quantise_cash(PACK, 0, 4)
        quantise_cash(PACK, 4, 6)

        for unit in range(1, UNITS):
            first = PACK + 2 * unit
            turning = first < TILES
            for t in range(PACK):
                if t == 1 and turning:
                    turn_cash(first, 2)
                    if unit == 1:
                        for tile in range(3 * PACK, TILES):
                            load_cash(tile)
                multiply(unit, t)
                subtract_fee(unit, t)
                if t == 0 and unit > 1:
                    quantise_y(unit - 2, 0, HALF)
            for t in range(PACK):
                clamp(unit, t, nc.gpsimd if t < ON_GPSIMD else nc.vector)
            share = OUT_SHARE if turning else 0
            if unit == 1:
                lay_cash(first)
            lay_y(unit - 1, share)
            if turning:
                if unit > 1:
                    lay_cash(first)
                for t in range(PACK):
                    scale_fee()
                interleave(nc.vector.tensor_copy, y_laid[unit - 1], y[unit - 1], 0, share)
                quantise_cash(first, 0, 4)
                quantise_cash(first, 4, 6)

        last = UNITS - 1
        lay_y(last, LAST_SHARE)
        interleave(nc.vector.tensor_copy, y_laid[last], y[last], 0, LAST_SHARE)
        quantise_y(last - 1, 0, HALF)
        quantise_y(last, 0, LAST_SHARE)
        quantise_y(last, LAST_SHARE, HALF)

        scale_rows = out_2.bitcast(I32)
        for q in range(P // QUADRANT):
            queue = nc.scalar if q < 2 else nc.sync
            queue.dma_start(out=scale_rows[:, PACK * q:PACK * (q + 1), :],
                            in_=y_scales[QUADRANT * q:QUADRANT * q + PACK * GROUPS, :].bitcast(I32))
